import numpy as np
import ml_dtypes


def mxq(x, axis, fmt="e4m3"):
    dtype, down = {"e4m3": (ml_dtypes.float8_e4m3fn, 7), "e5m2": (ml_dtypes.float8_e5m2, 14)}[fmt]
    v = np.moveaxis(np.asarray(x, np.float32).astype(ml_dtypes.bfloat16).astype(np.float64), axis, -1)
    blocks = v.reshape(v.shape[:-1] + (-1, 32))
    amax = np.abs(blocks).max(-1, keepdims=True)
    byte = np.maximum(np.where(amax > 0, np.frexp(amax)[1] - 1 + 127, 0) - down, 1)
    scale = np.exp2(byte - 127.0)
    codes = (blocks / scale).astype(np.float32).astype(dtype).astype(np.float64)
    return np.moveaxis((codes * scale).reshape(v.shape), -1, axis)


WIDE = False


def mx_kscale(k):
    if not WIDE:
        return np.ones(k)
    levels = np.array([10, -10, 5, -5, 0])
    if k % 512:
        return np.exp2(np.random.permutation(np.resize(levels, k // 32))).repeat(32)
    a = np.empty((k // 512, 16))
    for p in range(k // 512):
        a[p, :8] = np.random.permutation(np.resize(levels, 8))
        for g in range(8):
            far = levels[np.abs(levels - a[p, g]) >= 10]
            a[p, g + 8] = far[np.random.randint(len(far))]
    return np.exp2(a.ravel()).repeat(32)


def f64(x):
    return np.asarray(x).astype(np.float64)


def striped(idx):
    return np.tile(idx.reshape(-1, 16).T, (8, 1)).astype(np.uint16)


def unstriped(offs):
    return offs[:16].T.reshape(-1).astype(np.int64)


def striped8(idx):
    return np.concatenate([x.reshape(-1, 16).T for x in idx]).astype(np.uint16)


def runs(offs, k):
    lists = np.stack([offs[16 * r : 16 * r + 16].T.reshape(-1) for r in range(8)]).astype(np.int64)
    return lists[np.arange(k) % 512 // 64]


def pack_weight(w):
    k, n = w.shape
    w = f64(np.asarray(w, np.float32).astype(ml_dtypes.bfloat16)).reshape(k // 32, 32, n)
    amax = np.abs(w).max(1)
    byte = np.clip(np.where(amax > 0, np.frexp(amax)[1] - 1 + 127 - 7, 1), 1, 254)
    scaled = (w * np.exp2(127.0 - byte)[:, None, :]).reshape(k, n).astype(np.float32)
    words = np.ascontiguousarray(scaled.reshape(k // 512, 128, 4, n).transpose(0, 1, 3, 2)).astype(ml_dtypes.float8_e4m3fn).view(np.uint8)
    return words, np.ascontiguousarray(byte.astype(np.uint8).reshape(k // 512, 16, n))


def unpack_weight(words, scales):
    g, p, n, _ = words.shape
    vals = np.ascontiguousarray(words).view(ml_dtypes.float8_e4m3fn).astype(np.float64) * np.repeat(np.exp2(scales.astype(np.float64) - 127.0), 8, axis=1)[..., None]
    return vals.transpose(0, 1, 3, 2).reshape(g * 512, n)


K, T, S, N, H = 512, 2048, 512, 512, 512


def setup_inputs():
    n = np.random.standard_normal
    s = mx_kscale(K)[:, None]
    u = mx_kscale(S)
    packed_xT = pack_weight(n((K, T)) * s)
    return {
        "x_words": packed_xT[0],
        "x_scales": packed_xT[1],
        "wa": (n((K, H)) / np.sqrt(K) / s).astype(np.float32),
        "gt": (np.random.uniform(0.5, 1.5, (S, 1)) * u[:, None]).astype(np.float32),
        "w1": (n((S, N)) / np.sqrt(S) / u[:, None]).astype(np.float32),
        "offs": striped(np.random.permutation(T)[:S]),
        "fl": striped8(np.stack([np.random.permutation(H) for _ in range(8)])),
    }


def reference(x_words, x_scales, wa, gt, w1, offs, fl):
    xq = unpack_weight(x_words, x_scales)[:, unstriped(offs)]
    y = xq.T @ mxq(f64(wa), 0, "e4m3")
    z = f64(gt) * (y / (np.abs(y[np.arange(S)[:, None], runs(fl, S)]) + 0.5))
    return mxq(f64(w1), 0, "e4m3").T @ mxq(z, 0, "e4m3")

@@ -1,0 +1,187 @@
+from contextlib import ExitStack
+
+import concourse.mybir as mybir
+
+K, T, S, N, H = 512, 2048, 512, 512, 512
+FLOPS = 2 * S * K * H + 2 * N * S * H
+
+F32 = mybir.dt.float32
+BF16 = mybir.dt.bfloat16
+I32 = mybir.dt.int32
+U32 = mybir.dt.uint32
+U16 = mybir.dt.uint16
+U8 = mybir.dt.uint8
+FP8X4 = mybir.dt.float8_e4m3fn_x4
+AF = mybir.ActivationFunctionType
+MULT = mybir.AluOpType.mult
+
+P = 128
+PACK = 4
+HALF = 256
+RUN = 4
+WA_ON_SCALAR = (128)
+QUARTER = 128
+
+
+def interleave(copy, dst, src):
+    copy(dst.rearrange("p (c i) t -> p c t i", i=RUN), src.rearrange("p t (c i) -> p c t i", i=RUN))
+
+
+def tile_picked_featdev_none_p_kernel(tc, x_words, x_scales, wa, gt, w1, offs, fl, out):
+    nc = tc.nc
+    with ExitStack() as ctx:
+        sb = ctx.enter_context(tc.tile_pool(name="sb", bufs=1))
+        ps = ctx.enter_context(tc.psum_pool(name="ps", bufs=1))
+
+        def tile(name, shape, dtype):
+            return sb.tile(shape, dtype, name=name, align_bytes=64)
+
+        offs_sb = tile("offs_sb", [P, S // 16], U16)
+        fl_sb = tile("fl_sb", [P, H // 16], U16)
+        words = tile("words", [P, T], U32)
+        bytes_ = tile("scale_bytes", [P, T], U8)
+        four = tile("four", [P, 1], F32)
+        half = tile("half", [P, 1], F32)
+        gate = tile("gate", [P, PACK], F32)
+        wa_raw = [tile("wa_raw%d" % h, [P, PACK, HALF], F32) for h in range(2)]
+        w1_raw = [tile("w1_raw%d" % h, [P, PACK, HALF], F32) for h in range(2)]
+
+        nc.gpsimd.memset(bytes_[:].bitcast(I32), 0)
+        nc.gpsimd.memset(four[:], 4.0)
+
+        nc.sync.dma_start(offs_sb[:], offs)
+        for q in range(4):
+            nc.scalar.dma_start(bytes_[32 * q : 32 * q + 4, :].bitcast(I32), x_scales[0][4 * q : 4 * q + 4, :].bitcast(I32))
+        nc.sync.dma_start(words[:].bitcast(I32), x_words[0].rearrange("p c r -> p (c r)").bitcast(I32))
+        wa_rows = wa.rearrange("(p t) n -> p t n", t=PACK)
+        w1_rows = w1.rearrange("(p t) n -> p t n", t=PACK)
+        for h in range(2):
+            nc.sync.dma_start(wa_raw[h][:], wa_rows[:, :, h * HALF : (h + 1) * HALF])
+        for h in range(2):
+            nc.sync.dma_start(w1_raw[h][:], w1_rows[:, :, h * HALF : (h + 1) * HALF])
+        nc.sync.dma_start(fl_sb[:], fl)
+        nc.sync.dma_start(gate[:], gt.rearrange("(p t) o -> p (t o)", t=PACK))
+
+        nc.scalar.activation(half[:], four[:], AF.Abs_reciprocal_sqrt)
+
+        picked_bytes = tile("picked_bytes", [P, S], U8)
+        x_scale = tile("x_scale", [P, S], U8)
+        x_codes = tile("x_codes", [P, S], U32)
+        nc.vector.tensor_copy(picked_bytes[:], bytes_[:].indirect(offs_sb[:]))
+        nc.vector.tensor_copy(
+            x_scale[:].rearrange("p (t m) -> p t m", t=PACK), picked_bytes[:].rearrange("p (m t) -> p t m", t=PACK)
+        )
+        nc.vector.tensor_copy(x_codes[:].rearrange("p (t m) -> p m t", t=PACK), words[:].indirect(offs_sb[:]))
+
+        def quantise(name, grouped):
+            width = grouped.shape[1]
+            codes = tile(name + "_codes", [P, width], U32)
+            scales = tile(name + "_scales", [P, width], U8)
+            nc.vector.quantize_mx(out=codes[:].bitcast(FP8X4), scales=scales[:], in_=grouped[:].rearrange("p n t -> p (n t)"))
+            return codes, scales
+
+        def product(acc, stationary, cols, moving):
+            nc.tensor.matmul_mx(
+                out=acc,
+                lhsT=stationary[0][:, cols].bitcast(FP8X4),
+                lhsT_scale=stationary[1][:, cols],
+                rhs=moving[0][:].bitcast(FP8X4),
+                rhs_scale=moving[1][:],
+                start=True,
+                stop=True,
+            )
+
+        y = [ps.tile([P, H], F32, name="y%d" % t) for t in range(PACK)]
+        halves = [slice(0, HALF), slice(HALF, H)]
+        window = [tile("window%d" % t, [P, H], F32) for t in range(PACK)]
+        size = [tile("size%d" % t, [P, H], F32) for t in range(PACK)]
+        root = [tile("root%d" % t, [P, H], F32) for t in range(PACK)]
+        whole = slice(0, H)
+        units = [(0, halves[0]), (1, halves[0]), (0, halves[1]), (1, halves[1]), (2, whole), (3, whole)]
+
+        def reciprocal_step(i):
+            if 2 <= i:
+                t, cols = units[i - 2]
+                nc.scalar.activation(window[t][:, cols], root[t][:, cols], AF.Square)
+            if 1 <= i <= len(units):
+                t, cols = units[i - 1]
+                nc.scalar.activation(root[t][:, cols], size[t][:, cols], AF.Abs_reciprocal_sqrt, bias=half[:])
+            if i < len(units):
+                t, cols = units[i]
+                nc.scalar.activation(size[t][:, cols], y[t][:, cols], AF.Abs)
+
+
+        def project(h, grouped):
+            wa_q = quantise("wa%d" % h, grouped)
+            for t in range(PACK):
+                product(y[t][:, halves[h]], (x_codes, x_scale), slice(t * P, (t + 1) * P), wa_q)
+
+        wa_grouped = [tile("wa_bf16_%d" % h, [P, HALF, PACK], BF16) for h in range(2)]
+        interleave(nc.scalar.copy, wa_grouped[0][:], wa_raw[0][:])
+        project(0, wa_grouped[0])
+        interleave(nc.scalar.copy, wa_grouped[1][:, :WA_ON_SCALAR, :], wa_raw[1][:, :, :WA_ON_SCALAR])
+        interleave(nc.vector.tensor_copy, wa_grouped[1][:, WA_ON_SCALAR:, :], wa_raw[1][:, :, WA_ON_SCALAR:])
+        for i in range(2):
+            reciprocal_step(i)
+        project(1, wa_grouped[1])
+        for i in range(2, len(units) + 2):
+            reciprocal_step(i)
+
+        w1_grouped = [tile("w1_bf16_%d" % h, [P, HALF, PACK], BF16) for h in range(2)]
+        for h in range(2):
+            interleave(nc.vector.tensor_copy, w1_grouped[h][:], w1_raw[h][:])
+        w1_q = [quantise("w1%d" % h, w1_grouped[h]) for h in range(2)]
+
+        z = tile("z_rows", [P, PACK, H], BF16)
+
+        def fetch(name, t, cols):
+            fetched = tile(name, [P, cols.stop - cols.start], F32)
+            nc.vector.tensor_copy(fetched[:], window[t][:].indirect(fl_sb[:, cols.start // 16 : cols.stop // 16]))
+            return fetched
+
+        def divide(t, cols, fetched):
+            nc.vector.scalar_tensor_tensor(z[:, t, cols], y[t][:, cols], gate[:, t : t + 1], fetched[:], MULT, MULT)
+
+        out_rows = out.rearrange("(m p) j -> p m j", p=P)
+        quarters = [slice(c * QUARTER, (c + 1) * QUARTER) for c in range(4)]
+
+        def mix(c, z_q, bank, blocks, copy, queue):
+            acc = ps.tile([P, len(blocks), QUARTER], F32, name=bank)
+            for e, m in enumerate(blocks):
+                product(acc[:, e, :], w1_q[m // 2], slice(m % 2 * P, (m % 2 + 1) * P), z_q)
+            result = tile("result%d%d" % (c, blocks[0]), [P, len(blocks), QUARTER], F32)
+            copy(result[:], acc[:])
+            queue.dma_start(out_rows[:, blocks[0] : blocks[-1] + 1, quarters[c]], result[:])
+
+        def group(c, copy):
+            grouped = tile("z_bf16_%d" % c, [P, QUARTER, PACK], BF16)
+            interleave(copy, grouped[:], z[:, :, quarters[c]])
+            return grouped
+
+        last = PACK - 1
+        for t in range(last):
+            fetched = [fetch("fetched%d%d" % (t, h), t, halves[h]) for h in range(2)]
+            for h in range(2):
+                divide(t, halves[h], fetched[h])
+
+        f0 = fetch("f0", last, quarters[0])
+        f1 = fetch("f1", last, quarters[1])
+        divide(last, quarters[0], f0)
+        g0 = group(0, nc.scalar.copy)
+        f2 = fetch("f2", last, quarters[2])
+        divide(last, quarters[1], f1)
+        g1 = group(1, nc.scalar.copy)
+        divide(last, quarters[2], f2)
+        g2 = group(2, nc.scalar.copy)
+        q0 = quantise("z0", g0)
+        f3 = fetch("z_bf16_0", last, quarters[3])
+        mix(0, q0, "o0", [0, 1, 2, 3], nc.scalar.copy, nc.sync)
+        q1 = quantise("z1", g1)
+        divide(last, quarters[3], f3)
+        mix(1, q1, "o1", [0, 1, 2, 3], nc.scalar.copy, nc.sync)
+        q2 = quantise("z2", g2)
+        g3 = group(3, nc.vector.tensor_copy)
+        q3 = quantise("z3", g3)
+        mix(2, q2, "o2", [0, 1, 2, 3], nc.vector.tensor_copy, nc.sync)
+        mix(3, q3, "o3", [0, 1], nc.scalar.copy, nc.scalar)
+        mix(3, q3, "y0", [2, 3], nc.vector.tensor_copy, nc.sync)

@@ -19,7 +19,7 @@ P = 128
 PACK = 4
 HALF = 256
 RUN = 4
-WA_ON_SCALAR = (128)
+WA_ON_SCALAR = (160, 96)
 QUARTER = 128
 
 
@@ -46,20 +46,25 @@ def tile_picked_featdev_none_p_kernel(tc, x_words, x_scales, wa, gt, w1, offs, f
         wa_raw = [tile("wa_raw%d" % h, [P, PACK, HALF], F32) for h in range(2)]
         w1_raw = [tile("w1_raw%d" % h, [P, PACK, HALF], F32) for h in range(2)]
 
-        nc.gpsimd.memset(bytes_[:].bitcast(I32), 0)
+        zeroed = bytes_[:].bitcast(I32)
+        nc.vector.memset(zeroed[:, : T // 8], 0)
+        nc.gpsimd.memset(zeroed[:, T // 8 :], 0)
         nc.gpsimd.memset(four[:], 4.0)
 
+        x_rows = x_words[0].rearrange("p c r -> p (c r)").bitcast(I32)
         nc.sync.dma_start(offs_sb[:], offs)
         for q in range(4):
-            nc.scalar.dma_start(bytes_[32 * q : 32 * q + 4, :].bitcast(I32), x_scales[0][4 * q : 4 * q + 4, :].bitcast(I32))
-        nc.sync.dma_start(words[:].bitcast(I32), x_words[0].rearrange("p c r -> p (c r)").bitcast(I32))
+            (nc.sync, nc.scalar)[q % 2].dma_start(bytes_[32 * q : 32 * q + 4, :].bitcast(I32), x_scales[0][4 * q : 4 * q + 4, :].bitcast(I32))
+        for c in range(2):
+            cols = slice(c * T // 2, (c + 1) * T // 2)
+            nc.sync.dma_start(words[:, cols].bitcast(I32), x_rows[:, cols])
         wa_rows = wa.rearrange("(p t) n -> p t n", t=PACK)
         w1_rows = w1.rearrange("(p t) n -> p t n", t=PACK)
         for h in range(2):
             nc.sync.dma_start(wa_raw[h][:], wa_rows[:, :, h * HALF : (h + 1) * HALF])
+        nc.sync.dma_start(fl_sb[:], fl)
         for h in range(2):
             nc.sync.dma_start(w1_raw[h][:], w1_rows[:, :, h * HALF : (h + 1) * HALF])
-        nc.sync.dma_start(fl_sb[:], fl)
         nc.sync.dma_start(gate[:], gt.rearrange("(p t) o -> p (t o)", t=PACK))
 
         nc.scalar.activation(half[:], four[:], AF.Abs_reciprocal_sqrt)
@@ -68,14 +73,14 @@ def tile_picked_featdev_none_p_kernel(tc, x_words, x_scales, wa, gt, w1, offs, f
         x_scale = tile("x_scale", [P, S], U8)
         x_codes = tile("x_codes", [P, S], U32)
         nc.vector.tensor_copy(picked_bytes[:], bytes_[:].indirect(offs_sb[:]))
+        nc.vector.tensor_copy(x_codes[:].rearrange("p (t m) -> p m t", t=PACK), words[:].indirect(offs_sb[:]))
         nc.vector.tensor_copy(
             x_scale[:].rearrange("p (t m) -> p t m", t=PACK), picked_bytes[:].rearrange("p (m t) -> p t m", t=PACK)
         )
-        nc.vector.tensor_copy(x_codes[:].rearrange("p (t m) -> p m t", t=PACK), words[:].indirect(offs_sb[:]))
 
-        def quantise(name, grouped):
+        def quantise(name, grouped, buffer=None):
             width = grouped.shape[1]
-            codes = tile(name + "_codes", [P, width], U32)
+            codes = tile(buffer or name + "_codes", [P, width], U32)
             scales = tile(name + "_scales", [P, width], U8)
             nc.vector.quantize_mx(out=codes[:].bitcast(FP8X4), scales=scales[:], in_=grouped[:].rearrange("p n t -> p (n t)"))
             return codes, scales
@@ -93,54 +98,67 @@ def tile_picked_featdev_none_p_kernel(tc, x_words, x_scales, wa, gt, w1, offs, f
 
         y = [ps.tile([P, H], F32, name="y%d" % t) for t in range(PACK)]
         halves = [slice(0, HALF), slice(HALF, H)]
-        window = [tile("window%d" % t, [P, H], F32) for t in range(PACK)]
-        size = [tile("size%d" % t, [P, H], F32) for t in range(PACK)]
-        root = [tile("root%d" % t, [P, H], F32) for t in range(PACK)]
+        last = PACK - 1
         whole = slice(0, H)
-        units = [(0, halves[0]), (1, halves[0]), (0, halves[1]), (1, halves[1]), (2, whole), (3, whole)]
+        window = [tile("window%d" % t, [P, 2 * H if t < last else H], F32) for t in range(PACK)]
+        size = [window[t][:, H:] for t in range(last)] + [tile("late", [P, H], F32)[:]]
+        recip = tile("recip", [P, last, H], F32)
 
-        def reciprocal_step(i):
-            if 2 <= i:
-                t, cols = units[i - 2]
-                nc.scalar.activation(window[t][:, cols], root[t][:, cols], AF.Square)
-            if 1 <= i <= len(units):
-                t, cols = units[i - 1]
-                nc.scalar.activation(root[t][:, cols], size[t][:, cols], AF.Abs_reciprocal_sqrt, bias=half[:])
-            if i < len(units):
-                t, cols = units[i]
-                nc.scalar.activation(size[t][:, cols], y[t][:, cols], AF.Abs)
+        def magnitude(t, cols):
+            nc.scalar.activation(size[t][:, cols], y[t][:, cols], AF.Abs)
 
+        def inverse_root(t, cols):
+            nc.scalar.activation(window[t][:, cols], size[t][:, cols], AF.Abs_reciprocal_sqrt, bias=half[:])
 
-        def project(h, grouped):
-            wa_q = quantise("wa%d" % h, grouped)
-            for t in range(PACK):
-                product(y[t][:, halves[h]], (x_codes, x_scale), slice(t * P, (t + 1) * P), wa_q)
+        def fetch(dst, t, cols):
+            nc.vector.tensor_copy(dst, window[t][:].indirect(fl_sb[:, cols.start // 16 : cols.stop // 16]))
 
-        wa_grouped = [tile("wa_bf16_%d" % h, [P, HALF, PACK], BF16) for h in range(2)]
-        interleave(nc.scalar.copy, wa_grouped[0][:], wa_raw[0][:])
-        project(0, wa_grouped[0])
-        interleave(nc.scalar.copy, wa_grouped[1][:, :WA_ON_SCALAR, :], wa_raw[1][:, :, :WA_ON_SCALAR])
-        interleave(nc.vector.tensor_copy, wa_grouped[1][:, WA_ON_SCALAR:, :], wa_raw[1][:, :, WA_ON_SCALAR:])
-        for i in range(2):
-            reciprocal_step(i)
-        project(1, wa_grouped[1])
-        for i in range(2, len(units) + 2):
-            reciprocal_step(i)
+        def square(dst, src):
+            nc.scalar.activation(dst, src, AF.Square)
 
-        w1_grouped = [tile("w1_bf16_%d" % h, [P, HALF, PACK], BF16) for h in range(2)]
+        def divide(z, t, cols, factor):
+            nc.vector.scalar_tensor_tensor(z[:, t, :], y[t][:, cols], gate[:, t : t + 1], factor, MULT, MULT)
+
+        def project(t, h, wa_q):
+            product(y[t][:, halves[h]], (x_codes, x_scale), slice(t * P, (t + 1) * P), wa_q)
+
+        wa_q = []
         for h in range(2):
-            interleave(nc.vector.tensor_copy, w1_grouped[h][:], w1_raw[h][:])
-        w1_q = [quantise("w1%d" % h, w1_grouped[h]) for h in range(2)]
+            grouped = tile("wa_bf16_%d" % h, [P, HALF, PACK], BF16)
+            cut = WA_ON_SCALAR[h]
+            interleave(nc.scalar.copy, grouped[:, :cut, :], wa_raw[h][:, :, :cut])
+            interleave(nc.vector.tensor_copy, grouped[:, cut:, :], wa_raw[h][:, :, cut:])
+            wa_q.append(quantise("wa%d" % h, grouped))
+        project(0, 0, wa_q[0])
+        magnitude(0, halves[0])
+        project(0, 1, wa_q[1])
+        for t in range(1, PACK):
+            for h in range(2):
+                project(t, h, wa_q[h])
+        inverse_root(0, halves[0])
+        magnitude(0, halves[1])
+        magnitude(1, halves[0])
+        inverse_root(0, halves[1])
+        magnitude(1, halves[1])
+        for t in range(1, last):
+            magnitude(t + 1, whole)
+            inverse_root(t, whole)
+        inverse_root(last, whole)
 
-        z = tile("z_rows", [P, PACK, H], BF16)
+        def group(name, copy, rows):
+            grouped = tile(name, [P, rows.shape[2], PACK], BF16)
+            interleave(copy, grouped[:], rows)
+            return grouped
 
-        def fetch(name, t, cols):
-            fetched = tile(name, [P, cols.stop - cols.start], F32)
-            nc.vector.tensor_copy(fetched[:], window[t][:].indirect(fl_sb[:, cols.start // 16 : cols.stop // 16]))
-            return fetched
+        w1_first = quantise("w1_first", group("w1_first_bf16", nc.vector.tensor_copy, w1_raw[0][:]))
+        w1_second_bf16 = group("w1_second_bf16", nc.vector.tensor_copy, w1_raw[1][:])
+        fetched = tile("w1_raw1", [P, last, H], F32)
+        fetch(fetched[:, 0, :], 0, whole)
+        for t in range(1, last):
+            fetch(fetched[:, t, :], t, whole)
 
-        def divide(t, cols, fetched):
-            nc.vector.scalar_tensor_tensor(z[:, t, cols], y[t][:, cols], gate[:, t : t + 1], fetched[:], MULT, MULT)
+        fetched_last = tile("fetched_last", [P, HALF], F32)
+        fetch(fetched_last[:], last, halves[0])
 
         out_rows = out.rearrange("(m p) j -> p m j", p=P)
         quarters = [slice(c * QUARTER, (c + 1) * QUARTER) for c in range(4)]
@@ -153,35 +171,41 @@ def tile_picked_featdev_none_p_kernel(tc, x_words, x_scales, wa, gt, w1, offs, f
             copy(result[:], acc[:])
             queue.dma_start(out_rows[:, blocks[0] : blocks[-1] + 1, quarters[c]], result[:])
 
-        def group(c, copy):
-            grouped = tile("z_bf16_%d" % c, [P, QUARTER, PACK], BF16)
-            interleave(copy, grouped[:], z[:, :, quarters[c]])
-            return grouped
-
-        last = PACK - 1
-        for t in range(last):
-            fetched = [fetch("fetched%d%d" % (t, h), t, halves[h]) for h in range(2)]
-            for h in range(2):
-                divide(t, halves[h], fetched[h])
-
-        f0 = fetch("f0", last, quarters[0])
-        f1 = fetch("f1", last, quarters[1])
-        divide(last, quarters[0], f0)
-        g0 = group(0, nc.scalar.copy)
-        f2 = fetch("f2", last, quarters[2])
-        divide(last, quarters[1], f1)
-        g1 = group(1, nc.scalar.copy)
-        divide(last, quarters[2], f2)
-        g2 = group(2, nc.scalar.copy)
-        q0 = quantise("z0", g0)
-        f3 = fetch("z_bf16_0", last, quarters[3])
-        mix(0, q0, "o0", [0, 1, 2, 3], nc.scalar.copy, nc.sync)
-        q1 = quantise("z1", g1)
-        divide(last, quarters[3], f3)
-        mix(1, q1, "o1", [0, 1, 2, 3], nc.scalar.copy, nc.sync)
-        q2 = quantise("z2", g2)
-        g3 = group(3, nc.vector.tensor_copy)
-        q3 = quantise("z3", g3)
-        mix(2, q2, "o2", [0, 1, 2, 3], nc.vector.tensor_copy, nc.sync)
-        mix(3, q3, "o3", [0, 1], nc.scalar.copy, nc.scalar)
-        mix(3, q3, "y0", [2, 3], nc.vector.tensor_copy, nc.sync)
+        a, b = halves
+        every = list(range(N // P))
+        recip_a = [recip[:, 0, a], recip[:, 1, a], tile("handover", [P, HALF], F32)[:], tile("recip_a3", [P, HALF], F32)[:]]
+        square(recip[:, :2, a], fetched[:, :2, a])
+        square(recip_a[2], fetched[:, 2, a])
+        square(recip_a[3], fetched_last[:])
+        square(recip[:, :, b], fetched[:, :, b])
+        z_a = tile("z_a", [P, PACK, HALF], BF16)
+        for t in range(2):
+            divide(z_a, t, a, recip_a[t])
+        w1_q = [w1_first, quantise("w1_second", w1_second_bf16, "fetched_last")]
+        warm = ps.tile([P, H], F32, name="o1")
+        for e in range(2):
+            product(warm[:], w1_q[1], slice(e * P, (e + 1) * P), (x_codes, x_scale))
+        for t in range(2, PACK):
+            divide(z_a, t, a, recip_a[t])
+        z0 = group("z_first", nc.scalar.copy, z_a[:, :, :QUARTER])
+        fetched_last = tile("handover", [P, HALF], F32)
+        fetch(fetched_last[:], last, b)
+        z0 = quantise("z0", z0)
+        recip_last = tile("recip_b3", [P, HALF], F32)
+        square(recip_last[:], fetched_last[:])
+        z1 = group("z_second", nc.scalar.copy, z_a[:, :, QUARTER:])
+        mix(0, z0, "o0", every, nc.scalar.copy, nc.sync)
+        z_b = tile("z_first", [P, PACK, HALF], BF16)
+        divide(z_b, 0, b, recip[:, 0, b])
+        z1 = quantise("z1", z1)
+        mix(1, z1, "o1", every, nc.scalar.copy, nc.sync)
+        for t in range(1, last):
+            divide(z_b, t, b, recip[:, t, b])
+        divide(z_b, last, b, recip_last[:])
+        z2 = group("z_third", nc.vector.tensor_copy, z_b[:, :, :QUARTER])
+        z3 = group("z_fourth", nc.vector.tensor_copy, z_b[:, :, QUARTER:])
+        z2 = quantise("z2", z2)
+        z3 = quantise("z3", z3)
+        for c, z_q, banks in ((2, z2, ("o2", "o3")), (3, z3, ("y0", "y1"))):
+            mix(c, z_q, banks[0], every[:2], nc.scalar.copy, nc.scalar)
+            mix(c, z_q, banks[1], every[2:], nc.vector.tensor_copy, nc.sync)

from contextlib import ExitStack

import concourse.mybir as mybir

K, T, S, N, H = 512, 2048, 512, 512, 512
FLOPS = 2 * S * K * H + 2 * N * S * H

F32 = mybir.dt.float32
BF16 = mybir.dt.bfloat16
I32 = mybir.dt.int32
U32 = mybir.dt.uint32
U16 = mybir.dt.uint16
U8 = mybir.dt.uint8
FP8X4 = mybir.dt.float8_e4m3fn_x4
AF = mybir.ActivationFunctionType
MULT = mybir.AluOpType.mult

P = 128
PACK = 4
HALF = 256
RUN = 4
WA_ON_SCALAR = (160, 96)
QUARTER = 128


def interleave(copy, dst, src):
    copy(dst.rearrange("p (c i) t -> p c t i", i=RUN), src.rearrange("p t (c i) -> p c t i", i=RUN))


def tile_picked_featdev_none_p_kernel(tc, x_words, x_scales, wa, gt, w1, offs, fl, out):
    nc = tc.nc
    with ExitStack() as ctx:
        sb = ctx.enter_context(tc.tile_pool(name="sb", bufs=1))
        ps = ctx.enter_context(tc.psum_pool(name="ps", bufs=1))

        def tile(name, shape, dtype):
            return sb.tile(shape, dtype, name=name, align_bytes=64)

        offs_sb = tile("offs_sb", [P, S // 16], U16)
        fl_sb = tile("fl_sb", [P, H // 16], U16)
        words = tile("words", [P, T], U32)
        bytes_ = tile("scale_bytes", [P, T], U8)
        four = tile("four", [P, 1], F32)
        half = tile("half", [P, 1], F32)
        gate = tile("gate", [P, PACK], F32)
        wa_raw = [tile("wa_raw%d" % h, [P, PACK, HALF], F32) for h in range(2)]
        w1_raw = [tile("w1_raw%d" % h, [P, PACK, HALF], F32) for h in range(2)]

        zeroed = bytes_[:].bitcast(I32)
        nc.vector.memset(zeroed[:, : T // 8], 0)
        nc.gpsimd.memset(zeroed[:, T // 8 :], 0)
        nc.gpsimd.memset(four[:], 4.0)

        x_rows = x_words[0].rearrange("p c r -> p (c r)").bitcast(I32)
        nc.sync.dma_start(offs_sb[:], offs)
        for q in range(4):
            (nc.sync, nc.scalar)[q % 2].dma_start(bytes_[32 * q : 32 * q + 4, :].bitcast(I32), x_scales[0][4 * q : 4 * q + 4, :].bitcast(I32))
        for c in range(2):
            cols = slice(c * T // 2, (c + 1) * T // 2)
            nc.sync.dma_start(words[:, cols].bitcast(I32), x_rows[:, cols])
        wa_rows = wa.rearrange("(p t) n -> p t n", t=PACK)
        w1_rows = w1.rearrange("(p t) n -> p t n", t=PACK)
        for h in range(2):
            nc.sync.dma_start(wa_raw[h][:], wa_rows[:, :, h * HALF : (h + 1) * HALF])
        nc.sync.dma_start(fl_sb[:], fl)
        for h in range(2):
            nc.sync.dma_start(w1_raw[h][:], w1_rows[:, :, h * HALF : (h + 1) * HALF])
        nc.sync.dma_start(gate[:], gt.rearrange("(p t) o -> p (t o)", t=PACK))

        nc.scalar.activation(half[:], four[:], AF.Abs_reciprocal_sqrt)

        picked_bytes = tile("picked_bytes", [P, S], U8)
        x_scale = tile("x_scale", [P, S], U8)
        x_codes = tile("x_codes", [P, S], U32)
        nc.vector.tensor_copy(picked_bytes[:], bytes_[:].indirect(offs_sb[:]))
        nc.vector.tensor_copy(x_codes[:].rearrange("p (t m) -> p m t", t=PACK), words[:].indirect(offs_sb[:]))
        nc.vector.tensor_copy(
            x_scale[:].rearrange("p (t m) -> p t m", t=PACK), picked_bytes[:].rearrange("p (m t) -> p t m", t=PACK)
        )

        def quantise(name, grouped, buffer=None):
            width = grouped.shape[1]
            codes = tile(buffer or name + "_codes", [P, width], U32)
            scales = tile(name + "_scales", [P, width], U8)
            nc.vector.quantize_mx(out=codes[:].bitcast(FP8X4), scales=scales[:], in_=grouped[:].rearrange("p n t -> p (n t)"))
            return codes, scales

        def product(acc, stationary, cols, moving):
            nc.tensor.matmul_mx(
                out=acc,
                lhsT=stationary[0][:, cols].bitcast(FP8X4),
                lhsT_scale=stationary[1][:, cols],
                rhs=moving[0][:].bitcast(FP8X4),
                rhs_scale=moving[1][:],
                start=True,
                stop=True,
            )

        y = [ps.tile([P, H], F32, name="y%d" % t) for t in range(PACK)]
        halves = [slice(0, HALF), slice(HALF, H)]
        last = PACK - 1
        whole = slice(0, H)
        window = [tile("window%d" % t, [P, 2 * H if t < last else H], F32) for t in range(PACK)]
        size = [window[t][:, H:] for t in range(last)] + [tile("late", [P, H], F32)[:]]
        recip = tile("recip", [P, last, H], F32)

        def magnitude(t, cols):
            nc.scalar.activation(size[t][:, cols], y[t][:, cols], AF.Abs)

        def inverse_root(t, cols):
            nc.scalar.activation(window[t][:, cols], size[t][:, cols], AF.Abs_reciprocal_sqrt, bias=half[:])

        def fetch(dst, t, cols):
            nc.vector.tensor_copy(dst, window[t][:].indirect(fl_sb[:, cols.start // 16 : cols.stop // 16]))

        def square(dst, src):
            nc.scalar.activation(dst, src, AF.Square)

        def divide(z, t, cols, factor):
            nc.vector.scalar_tensor_tensor(z[:, t, :], y[t][:, cols], gate[:, t : t + 1], factor, MULT, MULT)

        def project(t, h, wa_q):
            product(y[t][:, halves[h]], (x_codes, x_scale), slice(t * P, (t + 1) * P), wa_q)

        wa_q = []
        for h in range(2):
            grouped = tile("wa_bf16_%d" % h, [P, HALF, PACK], BF16)
            cut = WA_ON_SCALAR[h]
            interleave(nc.scalar.copy, grouped[:, :cut, :], wa_raw[h][:, :, :cut])
            interleave(nc.vector.tensor_copy, grouped[:, cut:, :], wa_raw[h][:, :, cut:])
            wa_q.append(quantise("wa%d" % h, grouped))
        project(0, 0, wa_q[0])
        magnitude(0, halves[0])
        project(0, 1, wa_q[1])
        for t in range(1, PACK):
            for h in range(2):
                project(t, h, wa_q[h])
        inverse_root(0, halves[0])
        magnitude(0, halves[1])
        magnitude(1, halves[0])
        inverse_root(0, halves[1])
        magnitude(1, halves[1])
        for t in range(1, last):
            magnitude(t + 1, whole)
            inverse_root(t, whole)
        inverse_root(last, whole)

        def group(name, copy, rows):
            grouped = tile(name, [P, rows.shape[2], PACK], BF16)
            interleave(copy, grouped[:], rows)
            return grouped

        w1_first = quantise("w1_first", group("w1_first_bf16", nc.vector.tensor_copy, w1_raw[0][:]))
        w1_second_bf16 = group("w1_second_bf16", nc.vector.tensor_copy, w1_raw[1][:])
        fetched = tile("w1_raw1", [P, last, H], F32)
        fetch(fetched[:, 0, :], 0, whole)
        for t in range(1, last):
            fetch(fetched[:, t, :], t, whole)

        fetched_last = tile("fetched_last", [P, HALF], F32)
        fetch(fetched_last[:], last, halves[0])

        out_rows = out.rearrange("(m p) j -> p m j", p=P)
        quarters = [slice(c * QUARTER, (c + 1) * QUARTER) for c in range(4)]

        def mix(c, z_q, bank, blocks, copy, queue):
            acc = ps.tile([P, len(blocks), QUARTER], F32, name=bank)
            for e, m in enumerate(blocks):
                product(acc[:, e, :], w1_q[m // 2], slice(m % 2 * P, (m % 2 + 1) * P), z_q)
            result = tile("result%d%d" % (c, blocks[0]), [P, len(blocks), QUARTER], F32)
            copy(result[:], acc[:])
            queue.dma_start(out_rows[:, blocks[0] : blocks[-1] + 1, quarters[c]], result[:])

        a, b = halves
        every = list(range(N // P))
        recip_a = [recip[:, 0, a], recip[:, 1, a], tile("handover", [P, HALF], F32)[:], tile("recip_a3", [P, HALF], F32)[:]]
        square(recip[:, :2, a], fetched[:, :2, a])
        square(recip_a[2], fetched[:, 2, a])
        square(recip_a[3], fetched_last[:])
        square(recip[:, :, b], fetched[:, :, b])
        z_a = tile("z_a", [P, PACK, HALF], BF16)
        for t in range(2):
            divide(z_a, t, a, recip_a[t])
        w1_q = [w1_first, quantise("w1_second", w1_second_bf16, "fetched_last")]
        warm = ps.tile([P, H], F32, name="o1")
        for e in range(2):
            product(warm[:], w1_q[1], slice(e * P, (e + 1) * P), (x_codes, x_scale))
        for t in range(2, PACK):
            divide(z_a, t, a, recip_a[t])
        z0 = group("z_first", nc.scalar.copy, z_a[:, :, :QUARTER])
        fetched_last = tile("handover", [P, HALF], F32)
        fetch(fetched_last[:], last, b)
        z0 = quantise("z0", z0)
        recip_last = tile("recip_b3", [P, HALF], F32)
        square(recip_last[:], fetched_last[:])
        z1 = group("z_second", nc.scalar.copy, z_a[:, :, QUARTER:])
        mix(0, z0, "o0", every, nc.scalar.copy, nc.sync)
        z_b = tile("z_first", [P, PACK, HALF], BF16)
        divide(z_b, 0, b, recip[:, 0, b])
        z1 = quantise("z1", z1)
        mix(1, z1, "o1", every, nc.scalar.copy, nc.sync)
        for t in range(1, last):
            divide(z_b, t, b, recip[:, t, b])
        divide(z_b, last, b, recip_last[:])
        z2 = group("z_third", nc.vector.tensor_copy, z_b[:, :, :QUARTER])
        z3 = group("z_fourth", nc.vector.tensor_copy, z_b[:, :, QUARTER:])
        z2 = quantise("z2", z2)
        z3 = quantise("z3", z3)
        for c, z_q, banks in ((2, z2, ("o2", "o3")), (3, z3, ("y0", "y1"))):
            mix(c, z_q, banks[0], every[:2], nc.scalar.copy, nc.scalar)
            mix(c, z_q, banks[1], every[2:], nc.vector.tensor_copy, nc.sync)
